import numpy as np
import ml_dtypes


def mxq(x, axis, fmt="e4m3"):
    dtype, down = {"e4m3": (ml_dtypes.float8_e4m3fn, 7), "e5m2": (ml_dtypes.float8_e5m2, 14)}[fmt]
    v = np.moveaxis(np.asarray(x, np.float32).astype(ml_dtypes.bfloat16).astype(np.float64), axis, -1)
    blocks = v.reshape(v.shape[:-1] + (-1, 32))
    amax = np.abs(blocks).max(-1, keepdims=True)
    byte = np.maximum(np.where(amax > 0, np.frexp(amax)[1] - 1 + 127, 0) - down, 1)
    scale = np.exp2(byte - 127.0)
    codes = (blocks / scale).astype(np.float32).astype(dtype).astype(np.float64)
    return np.moveaxis((codes * scale).reshape(v.shape), -1, axis)


WIDE = False


def mx_kscale(k):
    if not WIDE:
        return np.ones(k)
    levels = np.array([30, -30])
    if k % 512:
        return np.exp2(np.random.permutation(np.resize(levels, k // 32))).repeat(32)
    a = np.empty((k // 512, 16))
    for p in range(k // 512):
        a[p, :8] = np.random.permutation(np.resize(levels, 8))
        for g in range(8):
            far = levels[np.abs(levels - a[p, g]) >= 10]
            a[p, g + 8] = far[np.random.randint(len(far))]
    return np.exp2(a.ravel()).repeat(32)


def f64(x):
    return np.asarray(x).astype(np.float64)


def striped(idx):
    return np.tile(np.asarray(idx).reshape(-1, 16).T, (8, 1)).astype(np.uint16)


def unstriped(offs):
    return offs[:16].T.reshape(-1).astype(np.int64)


E2M1 = np.array([0.0, 0.5, 1.0, 1.5, 2.0, 3.0, 4.0, 6.0, -0.0, -0.5, -1.0, -1.5, -2.0, -3.0, -4.0, -6.0])


def pack_weight(w, fmt):
    k, n = w.shape
    w = f64(np.asarray(w, np.float32).astype(ml_dtypes.bfloat16)).reshape(k // 32, 32, n)
    amax = np.abs(w).max(1)
    if fmt in ("e4m3", "e5m2"):
        byte = np.frexp(amax)[1] - 1 + 127 - (7 if fmt == "e4m3" else 14)
    else:
        mant, ex = np.frexp(amax / 6.0)
        byte = np.where(mant > 0.5, ex, ex - 1) + 127
    byte = np.clip(np.where(amax > 0, byte, 1), 1, 254)
    scaled = (w * np.exp2(127.0 - byte)[:, None, :]).reshape(k, n).astype(np.float32)
    by_word = np.ascontiguousarray(scaled.reshape(k // 512, 128, 4, n).transpose(0, 1, 3, 2))
    if fmt in ("e4m3", "e5m2"):
        words = by_word.astype(ml_dtypes.float8_e4m3fn if fmt == "e4m3" else ml_dtypes.float8_e5m2).view(np.uint8)
    else:
        c = by_word.astype(ml_dtypes.float4_e2m1fn).view(np.uint8) & 0xF
        words = (c[..., 0::2] | (c[..., 1::2] << 4)).reshape(k // 512, 128, 2 * n)
    return np.ascontiguousarray(words), np.ascontiguousarray(byte.astype(np.uint8).reshape(k // 512, 16, n))


def unpack_weight(words, scales, fmt):
    g, _, n = scales.shape
    words = np.ascontiguousarray(words).reshape(g, 128, n, -1)
    if fmt in ("e4m3", "e5m2"):
        vals = words.view(ml_dtypes.float8_e4m3fn if fmt == "e4m3" else ml_dtypes.float8_e5m2).astype(np.float64)
    else:
        nib = np.empty((g, 128, n, 4), np.uint8)
        nib[..., 0::2] = words & 0xF
        nib[..., 1::2] = words >> 4
        vals = E2M1[nib]
    vals = vals * np.repeat(np.exp2(scales.astype(np.float64) - 127.0), 8, axis=1)[..., None]
    return vals.transpose(0, 1, 3, 2).reshape(g * 512, n)


K, T, J, I, R, V = 512, 512, 256, 256, 512, 512


def setup_inputs():
    n = np.random.standard_normal
    idx = np.random.permutation(T)[:J]
    idx2 = np.random.permutation(V)[:J]
    idx3 = np.random.permutation(T)[:I]
    fk = mx_kscale(K)
    fr = mx_kscale(R)
    xtp = pack_weight(n((K, T)) / fk[:, None], "e2m1")
    wap = pack_weight(n((K, R)) * 0.5 / np.sqrt(K) * fk[:, None] * fr, "e5m2")
    wbp = pack_weight(n((K, R)) * 1 / np.sqrt(K) * fk[:, None] / fr, "e4m3")
    return {
        "xt_words": xtp[0],
        "xt_scales": xtp[1],
        "wa_words": wap[0],
        "wa_scales": wap[1],
        "tb": (n((R, V)) * 0.5 * fr[:, None]).astype(np.float32),
        "wb_words": wbp[0],
        "wb_scales": wbp[1],
        "offs": striped(idx),
        "offs2": striped(idx2),
        "offs3": striped(idx3),
    }


def reference(xt_words, xt_scales, wa_words, wa_scales, tb, wb_words, wb_scales, offs, offs2, offs3):
    idx = unstriped(offs)
    idx2 = unstriped(offs2)
    idx3 = unstriped(offs3)
    xtu = unpack_weight(xt_words, xt_scales, "e2m1")
    wau = unpack_weight(wa_words, wa_scales, "e5m2")
    wbu = unpack_weight(wb_words, wb_scales, "e4m3")
    xtidxg = xtu[:, idx]
    za = wau.T @ xtidxg
    ha = np.maximum(za - f64(tb)[:, idx2], 0.0)
    xtidx3g = xtu[:, idx3]
    zb = wbu.T @ xtidx3g
    kb1 = np.max(zb, axis=1, keepdims=True)
    hb = np.maximum(zb - 0.4 * kb1, 0.0)
    haq = mxq(ha, 0, "e5m2")
    hbq = mxq(hb, 0, "e5m2")
    a0 = haq.T @ hbq
    a1 = np.pad(a0, ((0, 0), (1, 0)))[:, :I]
    y = 0.04 * np.abs(a0 - a1)
    return y

@@ -1,0 +1,187 @@
+from contextlib import ExitStack
+
+import concourse.mybir as mybir
+
+K, T, J, I, R, V = 512, 512, 256, 256, 512, 512
+FLOPS = 2 * K * R * J + 2 * K * R * I + 2 * R * J * I
+
+F32 = mybir.dt.float32
+BF16 = mybir.dt.bfloat16
+I32 = mybir.dt.int32
+U32 = mybir.dt.uint32
+U16 = mybir.dt.uint16
+U8 = mybir.dt.uint8
+E4M3 = mybir.dt.float8_e4m3fn_x4
+E5M2 = mybir.dt.float8_e5m2_x4
+E2M1 = mybir.dt.float4_e2m1fn_x4
+ALU = mybir.AluOpType
+ACT = mybir.ActivationFunctionType
+
+P = 128
+SLOTS = 4
+RUN = 8
+HALVES = 2
+
+
+def load_scale_rows(queue, plane, rows):
+    for q in range(4):
+        queue.dma_start(out=plane[32 * q : 32 * q + 4, :].bitcast(I32), in_=rows[0, 4 * q : 4 * q + 4, :].bitcast(I32))
+
+
+def tile_list_meet_overtable_peakgated_steps_kernel(
+    tc, xt_words, xt_scales, wa_words, wa_scales, tb, wb_words, wb_scales, offs, offs2, offs3, out
+):
+    nc = tc.nc
+    with ExitStack() as ctx:
+        sb = ctx.enter_context(tc.tile_pool(name="sb", bufs=1))
+        ps = ctx.enter_context(tc.psum_pool(name="ps", bufs=1))
+
+        list_a = sb.tile([P, J // 16], U16, name="list_a")
+        list_tb = sb.tile([P, J // 16], U16, name="list_tb")
+        list_b = sb.tile([P, I // 16], U16, name="list_b")
+        x_words = sb.tile([P, T], U16, name="x_words", align_bytes=64)
+        x_plane = sb.tile([P, T], U8, name="x_plane", align_bytes=64)
+        wa_raw = sb.tile([P, R], U32, name="wa_raw", align_bytes=64)
+        wb_raw = sb.tile([P, R], U32, name="wb_raw", align_bytes=64)
+        wa_plane_raw = sb.tile([P, R], U8, name="wa_plane_raw", align_bytes=64)
+        wb_plane_raw = sb.tile([P, R], U8, name="wb_plane_raw", align_bytes=64)
+        tb_rows = [sb.tile([P, V], F32, name=f"tb_rows{t}", align_bytes=64) for t in range(SLOTS)]
+        before = [sb.tile([P, I], F32, name=f"before{h}", align_bytes=64) for h in range(HALVES)]
+
+        for plane in (x_plane, wb_plane_raw, wa_plane_raw):
+            nc.vector.memset(plane[:].bitcast(I32), 0)
+        for h in range(HALVES):
+            nc.vector.memset(before[h][:, 0:1], 0.0)
+
+        tb_by_slot = tb.rearrange("(g t e) v -> t g e v", t=SLOTS, e=RUN)
+        nc.sync.dma_start(list_b[:], offs3)
+        load_scale_rows(nc.scalar, x_plane, xt_scales)
+        nc.sync.dma_start(out=x_words[:].bitcast(I32), in_=xt_words[0].bitcast(I32))
+        nc.sync.dma_start(list_tb[:], offs2)
+        nc.sync.dma_start(out=tb_rows[0][:], in_=tb_by_slot[0])
+        nc.sync.dma_start(out=wb_raw[:].bitcast(I32), in_=wb_words[0].rearrange("p n t -> p (n t)").bitcast(I32))
+        load_scale_rows(nc.sync, wb_plane_raw, wb_scales)
+        nc.sync.dma_start(list_a[:], offs)
+        nc.sync.dma_start(out=wa_raw[:].bitcast(I32), in_=wa_words[0].rearrange("p n t -> p (n t)").bitcast(I32))
+        for t in range(1, SLOTS):
+            nc.sync.dma_start(out=tb_rows[t][:], in_=tb_by_slot[t])
+        load_scale_rows(nc.sync, wa_plane_raw, wa_scales)
+
+        def gather_tokens(name, offsets):
+            words = sb.tile([P, J], U16, name=name + "_words", align_bytes=64)
+            plane = sb.tile([P, J], U8, name=name + "_plane", align_bytes=64)
+            nc.vector.tensor_copy(words[:], x_words[:].indirect(offsets[:]))
+            nc.vector.tensor_copy(plane[:], x_plane[:].indirect(offsets[:]))
+            return words, plane
+
+        def deal_columns(name, raw, plane_raw):
+            words = sb.tile([P, R], U32, name=name + "_dealt", align_bytes=64)
+            plane = sb.tile([P, R], U8, name=name + "_plane", align_bytes=64)
+            nc.scalar.copy(
+                out=words[:].rearrange("p (t g e) -> p t g e", t=SLOTS, e=RUN),
+                in_=raw[:].rearrange("p (g t e) -> p t g e", t=SLOTS, e=RUN),
+            )
+            nc.scalar.copy(
+                out=plane[:].bitcast(U32).rearrange("p (t g e) -> p t g e", t=SLOTS, e=RUN // 4),
+                in_=plane_raw[:].bitcast(U32).rearrange("p (g t e) -> p t g e", t=SLOTS, e=RUN // 4),
+            )
+            return words, plane
+
+        tb_picked = sb.tile([P, SLOTS, J], F32, name="tb_picked", align_bytes=64)
+
+        def gather_tb(t):
+            nc.scalar.activation(tb_picked[:, t, :], tb_rows[t][:].indirect(list_tb[:]), ACT.Copy)
+
+        gather_tb(0)
+        xb_words, xb_plane = gather_tokens("xb", list_b)
+        wb_dealt, wb_plane = deal_columns("wb", wb_raw, wb_plane_raw)
+        xa_words, xa_plane = gather_tokens("xa", list_a)
+        gather_tb(1)
+        wa_dealt, wa_plane = deal_columns("wa", wa_raw, wa_plane_raw)
+
+        peak = sb.tile([P, SLOTS], F32, name="peak")
+        under = sb.tile([P, SLOTS, I], F32, name="under", align_bytes=64)
+        zb = [ps.tile([P, I], F32, name=f"zb{t}") for t in range(SLOTS)]
+        for t in range(SLOTS):
+            cols = slice(t * P, (t + 1) * P)
+            nc.tensor.matmul_mx(
+                out=zb[t][:],
+                lhsT=wb_dealt[:, cols].bitcast(E4M3),
+                lhsT_scale=wb_plane[:, cols],
+                rhs=xb_words[:].bitcast(E2M1),
+                rhs_scale=xb_plane[:],
+                start=True,
+                stop=True,
+            )
+            nc.vector.tensor_reduce(out=peak[:, t : t + 1], in_=zb[t][:], axis=mybir.AxisListType.X, op=ALU.max)
+            nc.scalar.activation(under[:, t, :], zb[t][:], ACT.Identity, bias=peak[:, t : t + 1], scale=-2.5)
+        gather_tb(2)
+        gather_tb(3)
+
+        za = [ps.tile([P, SLOTS, P], F32, name=f"za{h}") for h in range(HALVES)]
+        for h in range(HALVES):
+            rows = slice(h * P, (h + 1) * P)
+            for t in range(SLOTS):
+                cols = slice(t * P, (t + 1) * P)
+                nc.tensor.matmul_mx(
+                    out=za[h][:, t, :],
+                    lhsT=wa_dealt[:, cols].bitcast(E5M2),
+                    lhsT_scale=wa_plane[:, cols],
+                    rhs=xa_words[:, rows].bitcast(E2M1),
+                    rhs_scale=xa_plane[:, rows],
+                    start=True,
+                    stop=True,
+                )
+
+        hb = sb.tile([P, I, SLOTS], BF16, name="hb", align_bytes=64)
+        hb_words = sb.tile([P, I], U32, name="hb_words", align_bytes=64)
+        hb_plane = sb.tile([P, I], U8, name="hb_plane", align_bytes=64)
+        nc.vector.tensor_scalar(
+            out=hb[:].rearrange("p (c i) t -> p c t i", i=4),
+            in0=under[:].rearrange("p t (c i) -> p c t i", i=4),
+            scalar1=0.0,
+            scalar2=-0.4,
+            op0=ALU.min,
+            op1=ALU.mult,
+        )
+
+        excess = [sb.tile([P, SLOTS, P], F32, name=f"excess{h}", align_bytes=64) for h in range(HALVES)]
+        ha = [sb.tile([P, P, SLOTS], BF16, name=f"ha{h}", align_bytes=64) for h in range(HALVES)]
+        nc.vector.tensor_tensor(out=excess[0][:], in0=za[0][:], in1=tb_picked[:, :, 0:P], op=ALU.subtract)
+        nc.vector.quantize_mx(out=hb_words[:].bitcast(E5M2), scales=hb_plane[:], in_=hb[:].rearrange("p i t -> p (i t)"))
+        nc.scalar.activation(
+            ha[0][:].rearrange("p (c i) t -> p c t i", i=4),
+            excess[0][:].rearrange("p t (c i) -> p c t i", i=4),
+            ACT.Relu,
+        )
+        nc.vector.tensor_tensor(out=excess[1][:], in0=za[1][:], in1=tb_picked[:, :, P : 2 * P], op=ALU.subtract)
+        ha_words = [sb.tile([P, P], U32, name=f"ha_words{h}", align_bytes=64) for h in range(HALVES)]
+        ha_plane = [sb.tile([P, P], U8, name=f"ha_plane{h}", align_bytes=64) for h in range(HALVES)]
+        nc.vector.tensor_scalar(
+            out=ha[1][:].rearrange("p (c i) t -> p c t i", i=4),
+            in0=excess[1][:].rearrange("p t (c i) -> p c t i", i=4),
+            scalar1=0.0,
+            scalar2=None,
+            op0=ALU.max,
+        )
+        for h in range(HALVES):
+            nc.vector.quantize_mx(
+                out=ha_words[h][:].bitcast(E5M2), scales=ha_plane[h][:], in_=ha[h][:].rearrange("p j t -> p (j t)")
+            )
+        for h in range(HALVES):
+            score = ps.tile([P, I], F32, name=f"score{h}")
+            nc.tensor.matmul_mx(
+                out=score[:],
+                lhsT=ha_words[h][:].bitcast(E5M2),
+                lhsT_scale=ha_plane[h][:],
+                rhs=hb_words[:].bitcast(E5M2),
+                rhs_scale=hb_plane[:],
+                start=True,
+                stop=True,
+            )
+            step = sb.tile([P, I], F32, name=f"step{h}", align_bytes=64)
+            result = sb.tile([P, I], F32, name=f"result{h}", align_bytes=64)
+            nc.scalar.copy(out=before[h][:, 1:I], in_=score[:, 0 : I - 1])
+            nc.vector.tensor_tensor(out=step[:], in0=score[:], in1=before[h][:], op=ALU.subtract)
+            nc.scalar.activation(result[:], step[:], ACT.Abs, scale=0.04)
+            nc.sync.dma_start(out=out[h * P : (h + 1) * P, :], in_=result[:])

@@ -23,11 +23,6 @@ RUN = 8
 HALVES = 2
 
 
-def load_scale_rows(queue, plane, rows):
-    for q in range(4):
-        queue.dma_start(out=plane[32 * q : 32 * q + 4, :].bitcast(I32), in_=rows[0, 4 * q : 4 * q + 4, :].bitcast(I32))
-
-
 def tile_list_meet_overtable_peakgated_steps_kernel(
     tc, xt_words, xt_scales, wa_words, wa_scales, tb, wb_words, wb_scales, offs, offs2, offs3, out
 ):
@@ -44,62 +39,84 @@ def tile_list_meet_overtable_peakgated_steps_kernel(
         wa_raw = sb.tile([P, R], U32, name="wa_raw", align_bytes=64)
         wb_raw = sb.tile([P, R], U32, name="wb_raw", align_bytes=64)
         wa_plane_raw = sb.tile([P, R], U8, name="wa_plane_raw", align_bytes=64)
-        wb_plane_raw = sb.tile([P, R], U8, name="wb_plane_raw", align_bytes=64)
-        tb_rows = [sb.tile([P, V], F32, name=f"tb_rows{t}", align_bytes=64) for t in range(SLOTS)]
-        before = [sb.tile([P, I], F32, name=f"before{h}", align_bytes=64) for h in range(HALVES)]
+        wb_plane_raw = sb.tile([P, R], U8, name="wb_plane_raw", tag="plane_then_picked", align_bytes=64)
+        tb_rows = [sb.tile([P, V], F32, name=f"tb_rows{t}", tag=f"tb_rows{t}", align_bytes=64) for t in range(SLOTS)]
+        before = sb.tile([P, HALVES, I], F32, name="before", align_bytes=64)
 
-        for plane in (x_plane, wb_plane_raw, wa_plane_raw):
+        zero = sb.tile([P, HALVES], F32, name="zero")
+        nc.vector.memset(zero[:], 0.0)
+        for plane in (wb_plane_raw, wa_plane_raw):
             nc.vector.memset(plane[:].bitcast(I32), 0)
-        for h in range(HALVES):
-            nc.vector.memset(before[h][:, 0:1], 0.0)
 
         tb_by_slot = tb.rearrange("(g t e) v -> t g e v", t=SLOTS, e=RUN)
+
+        def load_words(tile, words):
+            nc.sync.dma_start(out=tile[:].bitcast(I32), in_=words[0].rearrange("p n t -> p (n t)").bitcast(I32))
+
+        def load_quadrant(queue, plane, rows, q):
+            queue.dma_start(out=plane[32 * q : 32 * q + 4, :].bitcast(I32), in_=rows[0, 4 * q : 4 * q + 4, :].bitcast(I32))
+
+        def load_x_quadrant(queue, q):
+            queue.dma_start(
+                out=x_plane[32 * q : 32 * q + 32, :].bitcast(I32),
+                in_=xt_scales[0, 4 * q : 4 * q + 4, :].bitcast(I32).partition_broadcast(8),
+            )
+
         nc.sync.dma_start(list_b[:], offs3)
-        load_scale_rows(nc.scalar, x_plane, xt_scales)
+        load_x_quadrant(nc.scalar, 0)
         nc.sync.dma_start(out=x_words[:].bitcast(I32), in_=xt_words[0].bitcast(I32))
-        nc.sync.dma_start(list_tb[:], offs2)
-        nc.sync.dma_start(out=tb_rows[0][:], in_=tb_by_slot[0])
-        nc.sync.dma_start(out=wb_raw[:].bitcast(I32), in_=wb_words[0].rearrange("p n t -> p (n t)").bitcast(I32))
-        load_scale_rows(nc.sync, wb_plane_raw, wb_scales)
+        load_x_quadrant(nc.scalar, 1)
+        load_x_quadrant(nc.sync, 2)
+        load_x_quadrant(nc.scalar, 3)
+        load_words(wb_raw, wb_words)
+        nc.scalar.dma_start(out=tb_rows[0][:], in_=tb_by_slot[0])
+        nc.scalar.activation(before[:, :, 0], zero[:], ACT.Copy)
+        load_quadrant(nc.gpsimd, wb_plane_raw, wb_scales, 3)
+        for q in range(2):
+            load_quadrant(nc.gpsimd, wa_plane_raw, wa_scales, q)
         nc.sync.dma_start(list_a[:], offs)
-        nc.sync.dma_start(out=wa_raw[:].bitcast(I32), in_=wa_words[0].rearrange("p n t -> p (n t)").bitcast(I32))
-        for t in range(1, SLOTS):
-            nc.sync.dma_start(out=tb_rows[t][:], in_=tb_by_slot[t])
-        load_scale_rows(nc.sync, wa_plane_raw, wa_scales)
+        nc.sync.dma_start(list_tb[:], offs2)
+        for q in range(3):
+            load_quadrant(nc.sync, wb_plane_raw, wb_scales, q)
+        nc.sync.dma_start(out=tb_rows[1][:], in_=tb_by_slot[1])
+        load_words(wa_raw, wa_words)
+        nc.sync.dma_start(out=tb_rows[2][:], in_=tb_by_slot[2])
+        for q in range(2, 4):
+            load_quadrant(nc.sync, wa_plane_raw, wa_scales, q)
+        nc.sync.dma_start(out=tb_rows[3][:], in_=tb_by_slot[3])
 
-        def gather_tokens(name, offsets):
-            words = sb.tile([P, J], U16, name=name + "_words", align_bytes=64)
-            plane = sb.tile([P, J], U8, name=name + "_plane", align_bytes=64)
-            nc.vector.tensor_copy(words[:], x_words[:].indirect(offsets[:]))
-            nc.vector.tensor_copy(plane[:], x_plane[:].indirect(offsets[:]))
-            return words, plane
-
-        def deal_columns(name, raw, plane_raw):
-            words = sb.tile([P, R], U32, name=name + "_dealt", align_bytes=64)
-            plane = sb.tile([P, R], U8, name=name + "_plane", align_bytes=64)
-            nc.scalar.copy(
-                out=words[:].rearrange("p (t g e) -> p t g e", t=SLOTS, e=RUN),
-                in_=raw[:].rearrange("p (g t e) -> p t g e", t=SLOTS, e=RUN),
+        def deal(copy, dealt, raw, run):
+            copy(
+                out=dealt.rearrange("p (t g e) -> p t g e", t=SLOTS, e=run),
+                in_=raw.rearrange("p (g t e) -> p t g e", t=SLOTS, e=run),
             )
-            nc.scalar.copy(
-                out=plane[:].bitcast(U32).rearrange("p (t g e) -> p t g e", t=SLOTS, e=RUN // 4),
-                in_=plane_raw[:].bitcast(U32).rearrange("p (g t e) -> p t g e", t=SLOTS, e=RUN // 4),
-            )
-            return words, plane
 
-        tb_picked = sb.tile([P, SLOTS, J], F32, name="tb_picked", align_bytes=64)
+        xb_words = sb.tile([P, I], U16, name="xb_words", align_bytes=64)
+        xb_plane = sb.tile([P, I], U8, name="xb_plane", align_bytes=64)
+        nc.vector.tensor_copy(xb_words[:], x_words[:].indirect(list_b[:]))
+        nc.vector.tensor_copy(xb_plane[:], x_plane[:].indirect(list_b[:]))
+        wb_dealt = sb.tile([P, R], U32, name="wb_dealt", align_bytes=64)
+        wb_plane = sb.tile([P, R], U8, name="wb_plane", align_bytes=64)
+        deal(nc.scalar.copy, wb_dealt[:], wb_raw[:], RUN)
+        xa_words = sb.tile([P, J], U16, name="xa_words", align_bytes=64)
+        nc.vector.tensor_copy(xa_words[:], x_words[:].indirect(list_a[:]))
+        deal(nc.vector.tensor_copy, wb_plane[:].bitcast(I32), wb_plane_raw[:].bitcast(I32), RUN // 4)
+        xa_plane = sb.tile([P, J], U8, name="xa_plane", tag="plane_then_picked", align_bytes=64)
+        nc.vector.tensor_copy(xa_plane[:], x_plane[:].indirect(list_a[:]))
+
+        tb_picked = [sb.tile([P, 2, J], F32, name="tb_picked0", align_bytes=64)]
 
         def gather_tb(t):
-            nc.scalar.activation(tb_picked[:, t, :], tb_rows[t][:].indirect(list_tb[:]), ACT.Copy)
+            nc.scalar.activation(tb_picked[t // 2][:, t % 2, :], tb_rows[t][:].indirect(list_tb[:]), ACT.Copy)
 
         gather_tb(0)
-        xb_words, xb_plane = gather_tokens("xb", list_b)
-        wb_dealt, wb_plane = deal_columns("wb", wb_raw, wb_plane_raw)
-        xa_words, xa_plane = gather_tokens("xa", list_a)
         gather_tb(1)
-        wa_dealt, wa_plane = deal_columns("wa", wa_raw, wa_plane_raw)
+        wa_dealt = sb.tile([P, R], U32, name="wa_dealt", align_bytes=64)
+        wa_plane = sb.tile([P, R], U8, name="wa_plane", align_bytes=64)
+        deal(nc.gpsimd.tensor_copy, wa_dealt[:], wa_raw[:], RUN)
+        deal(nc.gpsimd.tensor_copy, wa_plane[:].bitcast(U32), wa_plane_raw[:].bitcast(U32), RUN // 4)
 
-        peak = sb.tile([P, SLOTS], F32, name="peak")
+        peak = sb.tile([P, SLOTS], F32, name="peak", tag="peak_then_picked", align_bytes=64)
         under = sb.tile([P, SLOTS, I], F32, name="under", align_bytes=64)
         zb = [ps.tile([P, I], F32, name=f"zb{t}") for t in range(SLOTS)]
         for t in range(SLOTS):
@@ -115,6 +132,7 @@ def tile_list_meet_overtable_peakgated_steps_kernel(
             )
             nc.vector.tensor_reduce(out=peak[:, t : t + 1], in_=zb[t][:], axis=mybir.AxisListType.X, op=ALU.max)
             nc.scalar.activation(under[:, t, :], zb[t][:], ACT.Identity, bias=peak[:, t : t + 1], scale=-2.5)
+        tb_picked.append(sb.tile([P, 2, J], F32, name="tb_picked1", tag="peak_then_picked", align_bytes=64))
         gather_tb(2)
         gather_tb(3)
 
@@ -136,6 +154,16 @@ def tile_list_meet_overtable_peakgated_steps_kernel(
         hb = sb.tile([P, I, SLOTS], BF16, name="hb", align_bytes=64)
         hb_words = sb.tile([P, I], U32, name="hb_words", align_bytes=64)
         hb_plane = sb.tile([P, I], U8, name="hb_plane", align_bytes=64)
+        excess = [sb.tile([P, SLOTS, P], F32, name=f"excess{h}", align_bytes=64) for h in range(HALVES)]
+
+        def take_off_tb(h, u):
+            nc.vector.tensor_tensor(
+                out=excess[h][:, 2 * u : 2 * u + 2, :],
+                in0=za[h][:, 2 * u : 2 * u + 2, :],
+                in1=tb_picked[u][:, :, h * P : (h + 1) * P],
+                op=ALU.subtract,
+            )
+
         nc.vector.tensor_scalar(
             out=hb[:].rearrange("p (c i) t -> p c t i", i=4),
             in0=under[:].rearrange("p t (c i) -> p c t i", i=4),
@@ -145,16 +173,17 @@ def tile_list_meet_overtable_peakgated_steps_kernel(
             op1=ALU.mult,
         )
 
-        excess = [sb.tile([P, SLOTS, P], F32, name=f"excess{h}", align_bytes=64) for h in range(HALVES)]
         ha = [sb.tile([P, P, SLOTS], BF16, name=f"ha{h}", align_bytes=64) for h in range(HALVES)]
-        nc.vector.tensor_tensor(out=excess[0][:], in0=za[0][:], in1=tb_picked[:, :, 0:P], op=ALU.subtract)
+        take_off_tb(0, 0)
+        take_off_tb(1, 0)
+        take_off_tb(0, 1)
         nc.vector.quantize_mx(out=hb_words[:].bitcast(E5M2), scales=hb_plane[:], in_=hb[:].rearrange("p i t -> p (i t)"))
         nc.scalar.activation(
             ha[0][:].rearrange("p (c i) t -> p c t i", i=4),
             excess[0][:].rearrange("p t (c i) -> p c t i", i=4),
             ACT.Relu,
         )
-        nc.vector.tensor_tensor(out=excess[1][:], in0=za[1][:], in1=tb_picked[:, :, P : 2 * P], op=ALU.subtract)
+        take_off_tb(1, 1)
         ha_words = [sb.tile([P, P], U32, name=f"ha_words{h}", align_bytes=64) for h in range(HALVES)]
         ha_plane = [sb.tile([P, P], U8, name=f"ha_plane{h}", align_bytes=64) for h in range(HALVES)]
         nc.vector.tensor_scalar(
@@ -181,7 +210,7 @@ def tile_list_meet_overtable_peakgated_steps_kernel(
             )
             step = sb.tile([P, I], F32, name=f"step{h}", align_bytes=64)
             result = sb.tile([P, I], F32, name=f"result{h}", align_bytes=64)
-            nc.scalar.copy(out=before[h][:, 1:I], in_=score[:, 0 : I - 1])
-            nc.vector.tensor_tensor(out=step[:], in0=score[:], in1=before[h][:], op=ALU.subtract)
+            nc.scalar.copy(out=before[:, h, 1:I], in_=score[:, 0 : I - 1])
+            nc.vector.tensor_tensor(out=step[:], in0=score[:], in1=before[:, h, :], op=ALU.subtract)
             nc.scalar.activation(result[:], step[:], ACT.Abs, scale=0.04)
             nc.sync.dma_start(out=out[h * P : (h + 1) * P, :], in_=result[:])

@@ -50,8 +50,8 @@ def tile_list_meet_overtable_peakgated_steps_kernel(
 
         tb_by_slot = tb.rearrange("(g t e) v -> t g e v", t=SLOTS, e=RUN)
 
-        def load_words(tile, words):
-            nc.sync.dma_start(out=tile[:].bitcast(I32), in_=words[0].rearrange("p n t -> p (n t)").bitcast(I32))
+        def load_words(queue, tile, words):
+            queue.dma_start(out=tile[:].bitcast(I32), in_=words[0].rearrange("p n t -> p (n t)").bitcast(I32))
 
         def load_quadrant(queue, plane, rows, q):
             queue.dma_start(out=plane[32 * q : 32 * q + 4, :].bitcast(I32), in_=rows[0, 4 * q : 4 * q + 4, :].bitcast(I32))
@@ -68,22 +68,19 @@ def tile_list_meet_overtable_peakgated_steps_kernel(
         load_x_quadrant(nc.scalar, 1)
         load_x_quadrant(nc.sync, 2)
         load_x_quadrant(nc.scalar, 3)
-        load_words(wb_raw, wb_words)
-        nc.scalar.dma_start(out=tb_rows[0][:], in_=tb_by_slot[0])
+        load_words(nc.sync, wb_raw, wb_words)
+        load_words(nc.scalar, wa_raw, wa_words)
         nc.scalar.activation(before[:, :, 0], zero[:], ACT.Copy)
-        load_quadrant(nc.gpsimd, wb_plane_raw, wb_scales, 3)
-        for q in range(2):
-            load_quadrant(nc.gpsimd, wa_plane_raw, wa_scales, q)
         nc.sync.dma_start(list_a[:], offs)
-        nc.sync.dma_start(list_tb[:], offs2)
-        for q in range(3):
+        for q in range(4):
             load_quadrant(nc.sync, wb_plane_raw, wb_scales, q)
+        nc.sync.dma_start(out=tb_rows[0][:], in_=tb_by_slot[0])
+        nc.sync.dma_start(list_tb[:], offs2)
         nc.sync.dma_start(out=tb_rows[1][:], in_=tb_by_slot[1])
-        load_words(wa_raw, wa_words)
-        nc.sync.dma_start(out=tb_rows[2][:], in_=tb_by_slot[2])
-        for q in range(2, 4):
+        for q in range(4):
             load_quadrant(nc.sync, wa_plane_raw, wa_scales, q)
-        nc.sync.dma_start(out=tb_rows[3][:], in_=tb_by_slot[3])
+        for t in range(2, SLOTS):
+            nc.sync.dma_start(out=tb_rows[t][:], in_=tb_by_slot[t])
 
         def deal(copy, dealt, raw, run):
             copy(
@@ -95,30 +92,25 @@ def tile_list_meet_overtable_peakgated_steps_kernel(
         xb_plane = sb.tile([P, I], U8, name="xb_plane", align_bytes=64)
         nc.vector.tensor_copy(xb_words[:], x_words[:].indirect(list_b[:]))
         nc.vector.tensor_copy(xb_plane[:], x_plane[:].indirect(list_b[:]))
-        wb_dealt = sb.tile([P, R], U32, name="wb_dealt", align_bytes=64)
+        wb_dealt = sb.tile([P, R], U32, name="wb_dealt", tag="dealt_then_picked", align_bytes=64)
         wb_plane = sb.tile([P, R], U8, name="wb_plane", align_bytes=64)
         deal(nc.scalar.copy, wb_dealt[:], wb_raw[:], RUN)
+        wa_dealt = sb.tile([P, R], U32, name="wa_dealt", align_bytes=64)
+        deal(nc.scalar.copy, wa_dealt[:], wa_raw[:], RUN)
         xa_words = sb.tile([P, J], U16, name="xa_words", align_bytes=64)
         nc.vector.tensor_copy(xa_words[:], x_words[:].indirect(list_a[:]))
         deal(nc.vector.tensor_copy, wb_plane[:].bitcast(I32), wb_plane_raw[:].bitcast(I32), RUN // 4)
         xa_plane = sb.tile([P, J], U8, name="xa_plane", tag="plane_then_picked", align_bytes=64)
         nc.vector.tensor_copy(xa_plane[:], x_plane[:].indirect(list_a[:]))
 
-        tb_picked = [sb.tile([P, 2, J], F32, name="tb_picked0", align_bytes=64)]
-
-        def gather_tb(t):
-            nc.scalar.activation(tb_picked[t // 2][:, t % 2, :], tb_rows[t][:].indirect(list_tb[:]), ACT.Copy)
-
-        gather_tb(0)
-        gather_tb(1)
-        wa_dealt = sb.tile([P, R], U32, name="wa_dealt", align_bytes=64)
+        tb_first = sb.tile([P, 1, J], F32, name="tb_first", align_bytes=64)
+        nc.scalar.activation(tb_first[:, 0, :], tb_rows[0][:].indirect(list_tb[:]), ACT.Copy)
         wa_plane = sb.tile([P, R], U8, name="wa_plane", align_bytes=64)
-        deal(nc.gpsimd.tensor_copy, wa_dealt[:], wa_raw[:], RUN)
         deal(nc.gpsimd.tensor_copy, wa_plane[:].bitcast(U32), wa_plane_raw[:].bitcast(U32), RUN // 4)
 
-        peak = sb.tile([P, SLOTS], F32, name="peak", tag="peak_then_picked", align_bytes=64)
-        under = sb.tile([P, SLOTS, I], F32, name="under", align_bytes=64)
-        zb = [ps.tile([P, I], F32, name=f"zb{t}") for t in range(SLOTS)]
+        peak = sb.tile([P, SLOTS], F32, name="peak")
+        under = sb.tile([P, SLOTS, I], F32, name="under", tag="tb_rows0", align_bytes=64)
+        zb = [ps.tile([P, I], F32, name=f"zb{t}", tag=f"zb{t}") for t in range(SLOTS)]
         for t in range(SLOTS):
             cols = slice(t * P, (t + 1) * P)
             nc.tensor.matmul_mx(
@@ -130,11 +122,13 @@ def tile_list_meet_overtable_peakgated_steps_kernel(
                 start=True,
                 stop=True,
             )
-            nc.vector.tensor_reduce(out=peak[:, t : t + 1], in_=zb[t][:], axis=mybir.AxisListType.X, op=ALU.max)
-            nc.scalar.activation(under[:, t, :], zb[t][:], ACT.Identity, bias=peak[:, t : t + 1], scale=-2.5)
-        tb_picked.append(sb.tile([P, 2, J], F32, name="tb_picked1", tag="peak_then_picked", align_bytes=64))
-        gather_tb(2)
-        gather_tb(3)
+            nc.vector.tensor_reduce(out=peak[:, t : t + 1], in_=zb[t][:], axis=mybir.AxisListType.X, op=ALU.max, negate=True)
+            nc.scalar.activation(under[:, t, :], zb[t][:], ACT.Relu, bias=peak[:, t : t + 1], scale=2.5)
+        tb_second = sb.tile([P, 1, J], F32, name="tb_second", tag="dealt_then_picked", align_bytes=64)
+        nc.vector.tensor_copy(tb_second[:, 0, :], tb_rows[1][:].indirect(list_tb[:]))
+        tb_late = sb.tile([P, 2, J], F32, name="tb_late", tag="late_then_codes", align_bytes=64)
+        for t in range(2, SLOTS):
+            nc.scalar.activation(tb_late[:, t - 2, :], tb_rows[t][:].indirect(list_tb[:]), ACT.Copy)
 
         za = [ps.tile([P, SLOTS, P], F32, name=f"za{h}") for h in range(HALVES)]
         for h in range(HALVES):
@@ -152,40 +146,40 @@ def tile_list_meet_overtable_peakgated_steps_kernel(
                 )
 
         hb = sb.tile([P, I, SLOTS], BF16, name="hb", align_bytes=64)
-        hb_words = sb.tile([P, I], U32, name="hb_words", align_bytes=64)
         hb_plane = sb.tile([P, I], U8, name="hb_plane", align_bytes=64)
         excess = [sb.tile([P, SLOTS, P], F32, name=f"excess{h}", align_bytes=64) for h in range(HALVES)]
 
-        def take_off_tb(h, u):
+        def take_off_tb(h, slots, picked):
             nc.vector.tensor_tensor(
-                out=excess[h][:, 2 * u : 2 * u + 2, :],
-                in0=za[h][:, 2 * u : 2 * u + 2, :],
-                in1=tb_picked[u][:, :, h * P : (h + 1) * P],
+                out=excess[h][:, slots, :],
+                in0=za[h][:, slots, :],
+                in1=picked[:, :, h * P : (h + 1) * P],
                 op=ALU.subtract,
             )
 
         nc.vector.tensor_scalar(
             out=hb[:].rearrange("p (c i) t -> p c t i", i=4),
             in0=under[:].rearrange("p t (c i) -> p c t i", i=4),
-            scalar1=0.0,
-            scalar2=-0.4,
-            op0=ALU.min,
-            op1=ALU.mult,
+            scalar1=0.4,
+            scalar2=None,
+            op0=ALU.mult,
         )
 
         ha = [sb.tile([P, P, SLOTS], BF16, name=f"ha{h}", align_bytes=64) for h in range(HALVES)]
-        take_off_tb(0, 0)
-        take_off_tb(1, 0)
-        take_off_tb(0, 1)
-        nc.vector.quantize_mx(out=hb_words[:].bitcast(E5M2), scales=hb_plane[:], in_=hb[:].rearrange("p i t -> p (i t)"))
+        ha_words = [sb.tile([P, P], U32, name=f"ha_words{h}", align_bytes=64) for h in range(HALVES)]
+        ha_plane = [sb.tile([P, P], U8, name=f"ha_plane{h}", align_bytes=64) for h in range(HALVES)]
+        for h in range(HALVES):
+            take_off_tb(h, slice(0, 1), tb_first)
+            take_off_tb(h, slice(1, 2), tb_second)
+        for h in range(HALVES):
+            take_off_tb(h, slice(2, 4), tb_late)
         nc.scalar.activation(
             ha[0][:].rearrange("p (c i) t -> p c t i", i=4),
             excess[0][:].rearrange("p t (c i) -> p c t i", i=4),
             ACT.Relu,
         )
-        take_off_tb(1, 1)
-        ha_words = [sb.tile([P, P], U32, name=f"ha_words{h}", align_bytes=64) for h in range(HALVES)]
-        ha_plane = [sb.tile([P, P], U8, name=f"ha_plane{h}", align_bytes=64) for h in range(HALVES)]
+        hb_words = sb.tile([P, I], U32, name="hb_words", tag="late_then_codes", align_bytes=64)
+        nc.vector.quantize_mx(out=hb_words[:].bitcast(E5M2), scales=hb_plane[:], in_=hb[:].rearrange("p i t -> p (i t)"))
         nc.vector.tensor_scalar(
             out=ha[1][:].rearrange("p (c i) t -> p c t i", i=4),
             in0=excess[1][:].rearrange("p t (c i) -> p c t i", i=4),
@@ -198,19 +192,22 @@ def tile_list_meet_overtable_peakgated_steps_kernel(
                 out=ha_words[h][:].bitcast(E5M2), scales=ha_plane[h][:], in_=ha[h][:].rearrange("p j t -> p (j t)")
             )
         for h in range(HALVES):
-            score = ps.tile([P, I], F32, name=f"score{h}")
-            nc.tensor.matmul_mx(
-                out=score[:],
-                lhsT=ha_words[h][:].bitcast(E5M2),
-                lhsT_scale=ha_plane[h][:],
-                rhs=hb_words[:].bitcast(E5M2),
-                rhs_scale=hb_plane[:],
-                start=True,
-                stop=True,
-            )
             step = sb.tile([P, I], F32, name=f"step{h}", align_bytes=64)
             result = sb.tile([P, I], F32, name=f"result{h}", align_bytes=64)
-            nc.scalar.copy(out=before[:, h, 1:I], in_=score[:, 0 : I - 1])
-            nc.vector.tensor_tensor(out=step[:], in0=score[:], in1=before[:, h, :], op=ALU.subtract)
-            nc.scalar.activation(result[:], step[:], ACT.Abs, scale=0.04)
+            for c in range(2):
+                cols = slice(c * P, (c + 1) * P)
+                score = ps.tile([P, P], F32, name=f"score{h}{c}", tag=f"zb{2 * h + c}")
+                nc.tensor.matmul_mx(
+                    out=score[:],
+                    lhsT=ha_words[h][:].bitcast(E5M2),
+                    lhsT_scale=ha_plane[h][:],
+                    rhs=hb_words[:, cols].bitcast(E5M2),
+                    rhs_scale=hb_plane[:, cols],
+                    start=True,
+                    stop=True,
+                )
+                width = min(P, I - 1 - c * P)
+                nc.scalar.copy(out=before[:, h, c * P + 1 : c * P + 1 + width], in_=score[:, 0:width])
+                nc.vector.tensor_tensor(out=step[:, cols], in0=score[:], in1=before[:, h, cols], op=ALU.subtract)
+                nc.scalar.activation(result[:, cols], step[:, cols], ACT.Abs, scale=0.04)
             nc.sync.dma_start(out=out[h * P : (h + 1) * P, :], in_=result[:])

from contextlib import ExitStack

import concourse.mybir as mybir

K, T, J, I, R, V = 512, 512, 256, 256, 512, 512
FLOPS = 2 * K * R * J + 2 * K * R * I + 2 * R * J * I

F32 = mybir.dt.float32
BF16 = mybir.dt.bfloat16
I32 = mybir.dt.int32
U32 = mybir.dt.uint32
U16 = mybir.dt.uint16
U8 = mybir.dt.uint8
E4M3 = mybir.dt.float8_e4m3fn_x4
E5M2 = mybir.dt.float8_e5m2_x4
E2M1 = mybir.dt.float4_e2m1fn_x4
ALU = mybir.AluOpType
ACT = mybir.ActivationFunctionType

P = 128
SLOTS = 4
RUN = 8
HALVES = 2


def tile_list_meet_overtable_peakgated_steps_kernel(
    tc, xt_words, xt_scales, wa_words, wa_scales, tb, wb_words, wb_scales, offs, offs2, offs3, out
):
    nc = tc.nc
    with ExitStack() as ctx:
        sb = ctx.enter_context(tc.tile_pool(name="sb", bufs=1))
        ps = ctx.enter_context(tc.psum_pool(name="ps", bufs=1))

        list_a = sb.tile([P, J // 16], U16, name="list_a")
        list_tb = sb.tile([P, J // 16], U16, name="list_tb")
        list_b = sb.tile([P, I // 16], U16, name="list_b")
        x_words = sb.tile([P, T], U16, name="x_words", align_bytes=64)
        x_plane = sb.tile([P, T], U8, name="x_plane", align_bytes=64)
        wa_raw = sb.tile([P, R], U32, name="wa_raw", align_bytes=64)
        wb_raw = sb.tile([P, R], U32, name="wb_raw", align_bytes=64)
        wa_plane_raw = sb.tile([P, R], U8, name="wa_plane_raw", align_bytes=64)
        wb_plane_raw = sb.tile([P, R], U8, name="wb_plane_raw", tag="plane_then_picked", align_bytes=64)
        tb_rows = [sb.tile([P, V], F32, name=f"tb_rows{t}", tag=f"tb_rows{t}", align_bytes=64) for t in range(SLOTS)]
        before = sb.tile([P, HALVES, I], F32, name="before", align_bytes=64)

        zero = sb.tile([P, HALVES], F32, name="zero")
        nc.vector.memset(zero[:], 0.0)
        for plane in (wb_plane_raw, wa_plane_raw):
            nc.vector.memset(plane[:].bitcast(I32), 0)

        tb_by_slot = tb.rearrange("(g t e) v -> t g e v", t=SLOTS, e=RUN)

        def load_words(queue, tile, words):
            queue.dma_start(out=tile[:].bitcast(I32), in_=words[0].rearrange("p n t -> p (n t)").bitcast(I32))

        def load_quadrant(queue, plane, rows, q):
            queue.dma_start(out=plane[32 * q : 32 * q + 4, :].bitcast(I32), in_=rows[0, 4 * q : 4 * q + 4, :].bitcast(I32))

        def load_x_quadrant(queue, q):
            queue.dma_start(
                out=x_plane[32 * q : 32 * q + 32, :].bitcast(I32),
                in_=xt_scales[0, 4 * q : 4 * q + 4, :].bitcast(I32).partition_broadcast(8),
            )

        nc.sync.dma_start(list_b[:], offs3)
        load_x_quadrant(nc.scalar, 0)
        nc.sync.dma_start(out=x_words[:].bitcast(I32), in_=xt_words[0].bitcast(I32))
        load_x_quadrant(nc.scalar, 1)
        load_x_quadrant(nc.sync, 2)
        load_x_quadrant(nc.scalar, 3)
        load_words(nc.sync, wb_raw, wb_words)
        load_words(nc.scalar, wa_raw, wa_words)
        nc.scalar.activation(before[:, :, 0], zero[:], ACT.Copy)
        nc.sync.dma_start(list_a[:], offs)
        for q in range(4):
            load_quadrant(nc.sync, wb_plane_raw, wb_scales, q)
        nc.sync.dma_start(out=tb_rows[0][:], in_=tb_by_slot[0])
        nc.sync.dma_start(list_tb[:], offs2)
        nc.sync.dma_start(out=tb_rows[1][:], in_=tb_by_slot[1])
        for q in range(4):
            load_quadrant(nc.sync, wa_plane_raw, wa_scales, q)
        for t in range(2, SLOTS):
            nc.sync.dma_start(out=tb_rows[t][:], in_=tb_by_slot[t])

        def deal(copy, dealt, raw, run):
            copy(
                out=dealt.rearrange("p (t g e) -> p t g e", t=SLOTS, e=run),
                in_=raw.rearrange("p (g t e) -> p t g e", t=SLOTS, e=run),
            )

        xb_words = sb.tile([P, I], U16, name="xb_words", align_bytes=64)
        xb_plane = sb.tile([P, I], U8, name="xb_plane", align_bytes=64)
        nc.vector.tensor_copy(xb_words[:], x_words[:].indirect(list_b[:]))
        nc.vector.tensor_copy(xb_plane[:], x_plane[:].indirect(list_b[:]))
        wb_dealt = sb.tile([P, R], U32, name="wb_dealt", tag="dealt_then_picked", align_bytes=64)
        wb_plane = sb.tile([P, R], U8, name="wb_plane", align_bytes=64)
        deal(nc.scalar.copy, wb_dealt[:], wb_raw[:], RUN)
        wa_dealt = sb.tile([P, R], U32, name="wa_dealt", align_bytes=64)
        deal(nc.scalar.copy, wa_dealt[:], wa_raw[:], RUN)
        xa_words = sb.tile([P, J], U16, name="xa_words", align_bytes=64)
        nc.vector.tensor_copy(xa_words[:], x_words[:].indirect(list_a[:]))
        deal(nc.vector.tensor_copy, wb_plane[:].bitcast(I32), wb_plane_raw[:].bitcast(I32), RUN // 4)
        xa_plane = sb.tile([P, J], U8, name="xa_plane", tag="plane_then_picked", align_bytes=64)
        nc.vector.tensor_copy(xa_plane[:], x_plane[:].indirect(list_a[:]))

        tb_first = sb.tile([P, 1, J], F32, name="tb_first", align_bytes=64)
        nc.scalar.activation(tb_first[:, 0, :], tb_rows[0][:].indirect(list_tb[:]), ACT.Copy)
        wa_plane = sb.tile([P, R], U8, name="wa_plane", align_bytes=64)
        deal(nc.gpsimd.tensor_copy, wa_plane[:].bitcast(U32), wa_plane_raw[:].bitcast(U32), RUN // 4)

        peak = sb.tile([P, SLOTS], F32, name="peak")
        under = sb.tile([P, SLOTS, I], F32, name="under", tag="tb_rows0", align_bytes=64)
        zb = [ps.tile([P, I], F32, name=f"zb{t}", tag=f"zb{t}") for t in range(SLOTS)]
        for t in range(SLOTS):
            cols = slice(t * P, (t + 1) * P)
            nc.tensor.matmul_mx(
                out=zb[t][:],
                lhsT=wb_dealt[:, cols].bitcast(E4M3),
                lhsT_scale=wb_plane[:, cols],
                rhs=xb_words[:].bitcast(E2M1),
                rhs_scale=xb_plane[:],
                start=True,
                stop=True,
            )
            nc.vector.tensor_reduce(out=peak[:, t : t + 1], in_=zb[t][:], axis=mybir.AxisListType.X, op=ALU.max, negate=True)
            nc.scalar.activation(under[:, t, :], zb[t][:], ACT.Relu, bias=peak[:, t : t + 1], scale=2.5)
        tb_second = sb.tile([P, 1, J], F32, name="tb_second", tag="dealt_then_picked", align_bytes=64)
        nc.vector.tensor_copy(tb_second[:, 0, :], tb_rows[1][:].indirect(list_tb[:]))
        tb_late = sb.tile([P, 2, J], F32, name="tb_late", tag="late_then_codes", align_bytes=64)
        for t in range(2, SLOTS):
            nc.scalar.activation(tb_late[:, t - 2, :], tb_rows[t][:].indirect(list_tb[:]), ACT.Copy)

        za = [ps.tile([P, SLOTS, P], F32, name=f"za{h}") for h in range(HALVES)]
        for h in range(HALVES):
            rows = slice(h * P, (h + 1) * P)
            for t in range(SLOTS):
                cols = slice(t * P, (t + 1) * P)
                nc.tensor.matmul_mx(
                    out=za[h][:, t, :],
                    lhsT=wa_dealt[:, cols].bitcast(E5M2),
                    lhsT_scale=wa_plane[:, cols],
                    rhs=xa_words[:, rows].bitcast(E2M1),
                    rhs_scale=xa_plane[:, rows],
                    start=True,
                    stop=True,
                )

        hb = sb.tile([P, I, SLOTS], BF16, name="hb", align_bytes=64)
        hb_plane = sb.tile([P, I], U8, name="hb_plane", align_bytes=64)
        excess = [sb.tile([P, SLOTS, P], F32, name=f"excess{h}", align_bytes=64) for h in range(HALVES)]

        def take_off_tb(h, slots, picked):
            nc.vector.tensor_tensor(
                out=excess[h][:, slots, :],
                in0=za[h][:, slots, :],
                in1=picked[:, :, h * P : (h + 1) * P],
                op=ALU.subtract,
            )

        nc.vector.tensor_scalar(
            out=hb[:].rearrange("p (c i) t -> p c t i", i=4),
            in0=under[:].rearrange("p t (c i) -> p c t i", i=4),
            scalar1=0.4,
            scalar2=None,
            op0=ALU.mult,
        )

        ha = [sb.tile([P, P, SLOTS], BF16, name=f"ha{h}", align_bytes=64) for h in range(HALVES)]
        ha_words = [sb.tile([P, P], U32, name=f"ha_words{h}", align_bytes=64) for h in range(HALVES)]
        ha_plane = [sb.tile([P, P], U8, name=f"ha_plane{h}", align_bytes=64) for h in range(HALVES)]
        for h in range(HALVES):
            take_off_tb(h, slice(0, 1), tb_first)
            take_off_tb(h, slice(1, 2), tb_second)
        for h in range(HALVES):
            take_off_tb(h, slice(2, 4), tb_late)
        nc.scalar.activation(
            ha[0][:].rearrange("p (c i) t -> p c t i", i=4),
            excess[0][:].rearrange("p t (c i) -> p c t i", i=4),
            ACT.Relu,
        )
        hb_words = sb.tile([P, I], U32, name="hb_words", tag="late_then_codes", align_bytes=64)
        nc.vector.quantize_mx(out=hb_words[:].bitcast(E5M2), scales=hb_plane[:], in_=hb[:].rearrange("p i t -> p (i t)"))
        nc.vector.tensor_scalar(
            out=ha[1][:].rearrange("p (c i) t -> p c t i", i=4),
            in0=excess[1][:].rearrange("p t (c i) -> p c t i", i=4),
            scalar1=0.0,
            scalar2=None,
            op0=ALU.max,
        )
        for h in range(HALVES):
            nc.vector.quantize_mx(
                out=ha_words[h][:].bitcast(E5M2), scales=ha_plane[h][:], in_=ha[h][:].rearrange("p j t -> p (j t)")
            )
        for h in range(HALVES):
            step = sb.tile([P, I], F32, name=f"step{h}", align_bytes=64)
            result = sb.tile([P, I], F32, name=f"result{h}", align_bytes=64)
            for c in range(2):
                cols = slice(c * P, (c + 1) * P)
                score = ps.tile([P, P], F32, name=f"score{h}{c}", tag=f"zb{2 * h + c}")
                nc.tensor.matmul_mx(
                    out=score[:],
                    lhsT=ha_words[h][:].bitcast(E5M2),
                    lhsT_scale=ha_plane[h][:],
                    rhs=hb_words[:, cols].bitcast(E5M2),
                    rhs_scale=hb_plane[:, cols],
                    start=True,
                    stop=True,
                )
                width = min(P, I - 1 - c * P)
                nc.scalar.copy(out=before[:, h, c * P + 1 : c * P + 1 + width], in_=score[:, 0:width])
                nc.vector.tensor_tensor(out=step[:, cols], in0=score[:], in1=before[:, h, cols], op=ALU.subtract)
                nc.scalar.activation(result[:, cols], step[:, cols], ACT.Abs, scale=0.04)
            nc.sync.dma_start(out=out[h * P : (h + 1) * P, :], in_=result[:])
